import numpy as np
import ml_dtypes


def mxq(x, axis, fmt="e4m3"):
    dtype, down = {"e4m3": (ml_dtypes.float8_e4m3fn, 7), "e5m2": (ml_dtypes.float8_e5m2, 14)}[fmt]
    v = np.moveaxis(np.asarray(x, np.float32).astype(ml_dtypes.bfloat16).astype(np.float64), axis, -1)
    blocks = v.reshape(v.shape[:-1] + (-1, 32))
    amax = np.abs(blocks).max(-1, keepdims=True)
    byte = np.maximum(np.where(amax > 0, np.frexp(amax)[1] - 1 + 127, 0) - down, 1)
    scale = np.exp2(byte - 127.0)
    codes = (blocks / scale).astype(np.float32).astype(dtype).astype(np.float64)
    return np.moveaxis((codes * scale).reshape(v.shape), -1, axis)


WIDE = False


def mx_kscale(k):
    if not WIDE:
        return np.ones(k)
    levels = np.array([10, -10, 5, -5, 0])
    if k % 512:
        return np.exp2(np.random.permutation(np.resize(levels, k // 32))).repeat(32)
    a = np.empty((k // 512, 16))
    for p in range(k // 512):
        a[p, :8] = np.random.permutation(np.resize(levels, 8))
        for g in range(8):
            far = levels[np.abs(levels - a[p, g]) >= 10]
            a[p, g + 8] = far[np.random.randint(len(far))]
    return np.exp2(a.ravel()).repeat(32)


def f64(x):
    return np.asarray(x).astype(np.float64)


def striped(idx):
    return np.tile(np.asarray(idx).reshape(-1, 16).T, (8, 1)).astype(np.uint16)


def unstriped(offs):
    return offs[:16].T.reshape(-1).astype(np.int64)


E2M1 = np.array([0.0, 0.5, 1.0, 1.5, 2.0, 3.0, 4.0, 6.0, -0.0, -0.5, -1.0, -1.5, -2.0, -3.0, -4.0, -6.0])


def pack_weight(w, fmt):
    k, n = w.shape
    w = f64(np.asarray(w, np.float32).astype(ml_dtypes.bfloat16)).reshape(k // 32, 32, n)
    amax = np.abs(w).max(1)
    if fmt == "e4m3":
        byte = np.frexp(amax)[1] - 1 + 127 - 7
    else:
        mant, ex = np.frexp(amax / 6.0)
        byte = np.where(mant > 0.5, ex, ex - 1) + 127
    byte = np.clip(np.where(amax > 0, byte, 1), 1, 254)
    scaled = (w * np.exp2(127.0 - byte)[:, None, :]).reshape(k, n).astype(np.float32)
    by_word = np.ascontiguousarray(scaled.reshape(k // 512, 128, 4, n).transpose(0, 1, 3, 2))
    if fmt == "e4m3":
        words = by_word.astype(ml_dtypes.float8_e4m3fn).view(np.uint8)
    else:
        c = by_word.astype(ml_dtypes.float4_e2m1fn).view(np.uint8) & 0xF
        words = (c[..., 0::2] | (c[..., 1::2] << 4)).reshape(k // 512, 128, 2 * n)
    return np.ascontiguousarray(words), np.ascontiguousarray(byte.astype(np.uint8).reshape(k // 512, 16, n))


def unpack_weight(words, scales, fmt):
    g, _, n = scales.shape
    words = np.ascontiguousarray(words).reshape(g, 128, n, -1)
    if fmt == "e4m3":
        vals = words.view(ml_dtypes.float8_e4m3fn).astype(np.float64)
    else:
        nib = np.empty((g, 128, n, 4), np.uint8)
        nib[..., 0::2] = words & 0xF
        nib[..., 1::2] = words >> 4
        vals = E2M1[nib]
    vals = vals * np.repeat(np.exp2(scales.astype(np.float64) - 127.0), 8, axis=1)[..., None]
    return vals.transpose(0, 1, 3, 2).reshape(g * 512, n)


def sigmoid(v):
    return 1.0 / (1.0 + np.exp(-v))


K, T, J, B, N = 512, 2048, 2048, 512, 512


def setup_inputs():
    n = np.random.standard_normal
    idx = np.random.randint(0, T, J)
    fk = mx_kscale(K)
    wap = pack_weight(n((K, N)) * 1 / np.sqrt(K) * fk[:, None], "e2m1")
    xmp = pack_weight(n((K, J)) / fk[:, None], "e4m3")
    wmp = pack_weight(n((K, N)) * 1 / np.sqrt(K) * fk[:, None], "e2m1")
    return {
        "xf": (n((K, T))).astype(np.float32),
        "fk": (np.random.uniform(0.5, 2.0, (K, 1)) / fk[:, None]).astype(np.float32),
        "wa_words": wap[0],
        "wa_scales": wap[1],
        "xm_words": xmp[0],
        "xm_scales": xmp[1],
        "wm_words": wmp[0],
        "wm_scales": wmp[1],
        "offs": striped(idx),
    }


def reference(xf, fk, wa_words, wa_scales, xm_words, xm_scales, wm_words, wm_scales, offs):
    idx = unstriped(offs)
    wau = unpack_weight(wa_words, wa_scales, "e2m1")
    xmu = unpack_weight(xm_words, xm_scales, "e4m3")
    wmu = unpack_weight(wm_words, wm_scales, "e2m1")
    u = f64(xf)[:, idx].reshape(K, B, J // B).max(axis=2) * f64(fk)
    uq = mxq(u, 0, "e4m3")
    g = wau.T @ uq
    z = wmu.T @ xmu
    gr = np.repeat(g, J // B, axis=1)
    y = z * sigmoid(gr)
    return y

@@ -1,0 +1,199 @@
+from contextlib import ExitStack
+
+import concourse.mybir as mybir
+
+K, T, J, B, N = 512, 2048, 2048, 512, 512
+FLOPS = 2 * K * N * (B + J)
+
+F32 = mybir.dt.float32
+BF16 = mybir.dt.bfloat16
+I32 = mybir.dt.int32
+U32 = mybir.dt.uint32
+U16 = mybir.dt.uint16
+U8 = mybir.dt.uint8
+FP8X4 = mybir.dt.float8_e4m3fn_x4
+FP4X4 = mybir.dt.float4_e2m1fn_x4
+ALU = mybir.AluOpType
+ACT = mybir.ActivationFunctionType
+
+P = 128
+PACK = 4
+GROUP = J // B
+SLOTS = 512
+CHUNKS = J // SLOTS
+GROUPS = SLOTS // GROUP
+N_TILES = N // P
+LIST_COLS = SLOTS // 16
+
+
+def tile_list_group_expert_back_to_members_kernel(
+    tc, xf, fk, wa_words, wa_scales, xm_words, xm_scales, wm_words, wm_scales, offs, out
+):
+    nc = tc.nc
+    with ExitStack() as ctx:
+        held = ctx.enter_context(tc.tile_pool(name="held", bufs=1))
+        psum_g = ctx.enter_context(tc.psum_pool(name="psum_g", bufs=2))
+        psum_z = ctx.enter_context(tc.psum_pool(name="psum_z", bufs=6))
+
+        offsets = held.tile([P, J // 16], U16, name="offsets")
+        nc.sync.dma_start(offsets[:], offs)
+
+        wa_s = held.tile([P, N], U8, name="wa_s", align_bytes=64)
+        wm_s = held.tile([P, N], U8, name="wm_s", align_bytes=64)
+        xm_s = held.tile([P, J], U8, name="xm_s", align_bytes=64)
+        for plane in (wa_s, wm_s, xm_s):
+            nc.vector.memset(plane[:].bitcast(I32), 0)
+
+        def load_scale_rows(queue, plane, rows):
+            for q in range(4):
+                queue.dma_start(plane[32 * q : 32 * q + 4, :].bitcast(I32), rows[0, 4 * q : 4 * q + 4, :].bitcast(I32))
+
+        xf_rows = xf.rearrange("(p t) c -> p t c", t=PACK)
+        x = [held.tile([P, T], F32, name=f"x{t}") for t in range(PACK)]
+        for t in range(PACK):
+            nc.sync.dma_start(x[t][:], xf_rows[:, t, :])
+        fk_sb = held.tile([P, PACK], F32, name="fk_sb")
+        wa_w = held.tile([P, 2 * N], U8, name="wa_w", align_bytes=64)
+        wm_w = held.tile([P, 2 * N], U8, name="wm_w", align_bytes=64)
+        load_scale_rows(nc.gpsimd, wa_s, wa_scales)
+        nc.gpsimd.dma_start(fk_sb[:], fk.rearrange("(p t) o -> p (t o)", t=PACK))
+        nc.sync.dma_start(wa_w[:].bitcast(I32), wa_words[0].bitcast(I32))
+        nc.sync.dma_start(wm_w[:].bitcast(I32), wm_words[0].bitcast(I32))
+        load_scale_rows(nc.sync, xm_s, xm_scales)
+        xm_rows = xm_words[0].rearrange("p c r -> p (c r)").bitcast(I32)
+        xm_w = [held.tile([P, SLOTS], I32, name=f"xm_w{c}", tag=f"xm_w{c}", align_bytes=64) for c in range(CHUNKS)]
+        nc.sync.dma_start(xm_w[0][:], xm_rows[:, :SLOTS])
+        load_scale_rows(nc.sync, wm_s, wm_scales)
+        for c in range(1, CHUNKS):
+            nc.sync.dma_start(xm_w[c][:], xm_rows[:, c * SLOTS : (c + 1) * SLOTS])
+
+        largest = held.tile([P, CHUNKS, PACK, GROUPS], F32, name="largest")
+
+        def gather(engine, dst, t, c, first=0, last=LIST_COLS):
+            picked = x[t][:].indirect(offsets[:, c * LIST_COLS + first : c * LIST_COLS + last])
+            if engine == "scalar":
+                nc.scalar.activation(out=dst, in_=picked, func=ACT.Copy)
+            else:
+                nc.vector.tensor_copy(out=dst, in_=picked)
+
+        def max_of_halves(dst, src):
+            quads = src.rearrange("p (b m) -> p b m", m=GROUP)
+            nc.vector.tensor_tensor(
+                out=dst.rearrange("p (b m) -> p b m", m=2), in0=quads[:, :, 0:2], in1=quads[:, :, 2:4], op=ALU.max
+            )
+
+        def max_of_pairs(dst, src):
+            pairs = src.rearrange("p (r b m) -> p r b m", r=dst.shape[1], m=2)
+            nc.vector.tensor_tensor(out=dst, in0=pairs[:, :, :, 0], in1=pairs[:, :, :, 1], op=ALU.max)
+
+        def early(t, chunks, engine):
+            picked = held.tile([P, len(chunks) * SLOTS], F32, name=f"picked_{t}_{chunks[0]}")
+            halves = held.tile([P, len(chunks) * SLOTS // 2], F32, name=f"halves_{t}_{chunks[0]}")
+            for s, c in enumerate(chunks):
+                gather(engine, picked[:, s * SLOTS : (s + 1) * SLOTS], t, c)
+            max_of_halves(halves[:], picked[:])
+            max_of_pairs(largest[:, chunks[0] : chunks[-1] + 1, t, :], halves[:])
+
+        def late_gather(t, c, tag, engine="scalar"):
+            picked = held.tile([P, SLOTS], F32, name=f"picked_{t}_{c}", tag=tag, align_bytes=64)
+            gather(engine, picked[:], t, c)
+            return picked
+
+        def late_max(c, first, picked, tag):
+            halves = held.tile([P, len(picked) * SLOTS // 2], F32, name=f"halves_late{c}_{first}", tag=tag, align_bytes=64)
+            for s in range(len(picked)):
+                max_of_halves(halves[:, s * SLOTS // 2 : (s + 1) * SLOTS // 2], picked[s][:])
+            max_of_pairs(largest[:, c, first : first + len(picked), :], halves[:])
+
+        def expert(c, u_tag=None):
+            u = held.tile([P, GROUPS * PACK], BF16, name=f"u{c}", tag=f"u{c}", align_bytes=64)
+            nc.vector.tensor_tensor(
+                out=u[:].rearrange("p (d i t) -> p d t i", i=2, t=PACK),
+                in0=largest[:, c, :, :].rearrange("p t (d i) -> p d t i", i=2),
+                in1=fk_sb[:].unsqueeze(1).unsqueeze(3).to_broadcast([P, GROUPS // 2, PACK, 2]),
+                op=ALU.mult,
+            )
+            u_w = held.tile([P, GROUPS], U32, name=f"u_w{c}", tag=u_tag or f"u_w{c}", align_bytes=64)
+            u_s = held.tile([P, GROUPS], U8, name=f"u_s{c}", tag=f"u_s{c}", align_bytes=64)
+            nc.vector.quantize_mx(out=u_w[:].bitcast(FP8X4), scales=u_s[:], in_=u[:])
+            g = psum_g.tile([P, N_TILES, GROUPS], F32, name="g")
+            for i in range(N_TILES):
+                nc.tensor.matmul_mx(
+                    out=g[:, i, :],
+                    lhsT=wa_w[:, 2 * P * i : 2 * P * (i + 1)].bitcast(FP4X4),
+                    lhsT_scale=wa_s[:, P * i : P * (i + 1)],
+                    rhs=u_w[:].bitcast(FP8X4),
+                    rhs_scale=u_s[:],
+                    start=True,
+                    stop=True,
+                )
+            gates = []
+            for h in range(2):
+                gate = held.tile([P, 2, GROUPS], F32, name=f"gate{c}_{h}", tag=f"gate{c}_{h}", align_bytes=64)
+                nc.scalar.activation(out=gate[:], in_=g[:, 2 * h : 2 * h + 2, :], func=ACT.Sigmoid)
+                gates.append(gate)
+            return gates
+
+        out_rows = out.rearrange("(i p) j -> p i j", p=P)
+
+        def member_products(c):
+            words = xm_w[c][:]
+            banks = []
+            for i in range(N_TILES):
+                z = psum_z.tile([P, SLOTS], F32, name="z")
+                banks.append(z)
+                nc.tensor.matmul_mx(
+                    out=z[:],
+                    lhsT=wm_w[:, 2 * P * i : 2 * P * (i + 1)].bitcast(FP4X4),
+                    lhsT_scale=wm_s[:, P * i : P * (i + 1)],
+                    rhs=words.bitcast(FP8X4),
+                    rhs_scale=xm_s[:, c * SLOTS : (c + 1) * SLOTS],
+                    start=True,
+                    stop=True,
+                )
+            return banks
+
+        def members(c, h, gates, banks, per_store=2):
+            y = held.tile([P, 2, SLOTS], F32, name=f"y{c}_{h}")
+            for r in range(2):
+                nc.vector.tensor_tensor(
+                    out=y[:, r, :].rearrange("p (b m) -> p b m", m=GROUP),
+                    in0=banks[2 * h + r][:].rearrange("p (b m) -> p b m", m=GROUP),
+                    in1=gates[h][:, r, :].unsqueeze(2).to_broadcast([P, GROUPS, GROUP]),
+                    op=ALU.mult,
+                )
+                if (r + 1) % per_store == 0:
+                    first = r + 1 - per_store
+                    nc.sync.dma_start(
+                        out_rows[:, 2 * h + first : 2 * h + r + 1, c * SLOTS : (c + 1) * SLOTS], y[:, first : r + 1, :]
+                    )
+
+        early(0, [0, 1], "scalar")
+        early(0, [2, 3], "vector")
+        early(1, [0, 1], "scalar")
+        picked2 = [late_gather(1, 2, "p12", "vector")]
+        picked0 = [late_gather(2, 0, "p20")]
+        picked1 = [late_gather(2, 1, "p21")]
+        shared = held.tile([P, SLOTS], F32, name="picked_3_0", tag="p30", align_bytes=64)
+        gather("scalar", shared[:, : SLOTS // 2], 3, 0, 0, LIST_COLS // 2)
+        gather("vector", shared[:, SLOTS // 2 :], 3, 0, LIST_COLS // 2, LIST_COLS)
+        late_max(0, 2, picked0 + [shared], "h0")
+        picked1.append(late_gather(3, 1, "p31"))
+        picked2.append(late_gather(2, 2, "p30"))
+        last2 = late_gather(3, 2, "p32")
+        gate0 = expert(0)
+        late_max(1, 2, picked1, "h0")
+        late_max(2, 1, picked2, "h0")
+        z0 = member_products(0)
+        members(0, 0, gate0, z0)
+        gate1 = expert(1, "gate0_0")
+        late_max(2, 3, [last2], "u1")
+        gate2 = expert(2)
+        members(0, 1, gate0, z0)
+        picked3 = [late_gather(1, 3, "p30"), late_gather(2, 3, "p12"), late_gather(3, 3, "h0")]
+        late_max(3, 1, picked3, "gate0_1")
+        gate3 = expert(3)
+        for c, gates in ((1, gate1), (2, gate2), (3, gate3)):
+            z = member_products(c)
+            members(c, 0, gates, z)
+            members(c, 1, gates, z, 1 if c == CHUNKS - 1 else 2)

@@ -38,6 +38,11 @@ def tile_list_group_expert_back_to_members_kernel(
         offsets = held.tile([P, J // 16], U16, name="offsets")
         nc.sync.dma_start(offsets[:], offs)
 
+        warm_in = held.tile([P, 1], F32, name="warm_in")
+        warm_out = held.tile([P, 1], F32, name="warm_out")
+        nc.vector.memset(warm_in[:], 0.0)
+        nc.scalar.activation(out=warm_out[:], in_=warm_in[:], func=ACT.Sigmoid)
+
         wa_s = held.tile([P, N], U8, name="wa_s", align_bytes=64)
         wm_s = held.tile([P, N], U8, name="wm_s", align_bytes=64)
         xm_s = held.tile([P, J], U8, name="xm_s", align_bytes=64)

@@ -112,12 +112,27 @@ def tile_list_group_expert_back_to_members_kernel(
 
         def expert(c, u_tag=None):
             u = held.tile([P, GROUPS * PACK], BF16, name=f"u{c}", tag=f"u{c}", align_bytes=64)
-            nc.vector.tensor_tensor(
-                out=u[:].rearrange("p (d i t) -> p d t i", i=2, t=PACK),
-                in0=largest[:, c, :, :].rearrange("p t (d i) -> p d t i", i=2),
-                in1=fk_sb[:].unsqueeze(1).unsqueeze(3).to_broadcast([P, GROUPS // 2, PACK, 2]),
-                op=ALU.mult,
-            )
+            if c < 2:
+                nc.vector.tensor_tensor(
+                    out=u[:].rearrange("p (d i t) -> p d t i", i=2, t=PACK),
+                    in0=largest[:, c, :, :].rearrange("p t (d i) -> p d t i", i=2),
+                    in1=fk_sb[:].unsqueeze(1).unsqueeze(3).to_broadcast([P, GROUPS // 2, PACK, 2]),
+                    op=ALU.mult,
+                )
+            elif c == 3:
+                planes = held.tile([P, PACK, GROUPS], BF16, name="planes", tag="p32", align_bytes=64)
+                for t in range(PACK):
+                    nc.scalar.activation(
+                        out=planes[:, t, :], in_=largest[:, c, t, :], func=ACT.Copy, scale=fk_sb[:, t : t + 1]
+                    )
+                nc.scalar.copy(out=u[:].rearrange("p (b t) -> p b t", t=PACK), in_=planes[:].rearrange("p t b -> p b t"))
+            else:
+                nc.gpsimd.tensor_tensor(
+                    out=u[:].rearrange("p (b t) -> p b t", t=PACK),
+                    in0=largest[:, c, :, :].rearrange("p t b -> p b t"),
+                    in1=fk_sb[:].unsqueeze(1).to_broadcast([P, GROUPS, PACK]),
+                    op=ALU.mult,
+                )
             u_w = held.tile([P, GROUPS], U32, name=f"u_w{c}", tag=u_tag or f"u_w{c}", align_bytes=64)
             u_s = held.tile([P, GROUPS], U8, name=f"u_s{c}", tag=f"u_s{c}", align_bytes=64)
             nc.vector.quantize_mx(out=u_w[:].bitcast(FP8X4), scales=u_s[:], in_=u[:])
@@ -133,10 +148,10 @@ def tile_list_group_expert_back_to_members_kernel(
                     stop=True,
                 )
             gates = []
-            for h in range(2):
-                gate = held.tile([P, 2, GROUPS], F32, name=f"gate{c}_{h}", tag=f"gate{c}_{h}", align_bytes=64)
-                nc.scalar.activation(out=gate[:], in_=g[:, 2 * h : 2 * h + 2, :], func=ACT.Sigmoid)
-                gates.append(gate)
+            for h, (first, last) in enumerate(((0, 2), (2, N_TILES))):
+                gate = held.tile([P, last - first, GROUPS], F32, name=f"gate{c}_{h}", tag=f"gate{c}_{h}", align_bytes=64)
+                nc.scalar.activation(out=gate[:], in_=g[:, first:last, :], func=ACT.Sigmoid)
+                gates.extend(gate[:, r, :] for r in range(last - first))
             return gates
 
         out_rows = out.rearrange("(i p) j -> p i j", p=P)
@@ -158,20 +173,26 @@ def tile_list_group_expert_back_to_members_kernel(
                 )
             return banks
 
-        def members(c, h, gates, banks, per_store=2):
-            y = held.tile([P, 2, SLOTS], F32, name=f"y{c}_{h}")
-            for r in range(2):
+        y = {}
+        y_tags = {(1, 0): "gate0_0"}
+
+        def members(c, tiles, gates, banks):
+            for i in tiles:
+                h, r = divmod(i, 2)
+                if (c, h) not in y:
+                    tag = y_tags.get((c, h), f"y{c}_{h}")
+                    y.setdefault((c, h), held.tile([P, 2, SLOTS], F32, name=f"y{c}_{h}", tag=tag, align_bytes=64))
                 nc.vector.tensor_tensor(
-                    out=y[:, r, :].rearrange("p (b m) -> p b m", m=GROUP),
-                    in0=banks[2 * h + r][:].rearrange("p (b m) -> p b m", m=GROUP),
-                    in1=gates[h][:, r, :].unsqueeze(2).to_broadcast([P, GROUPS, GROUP]),
+                    out=y[c, h][:, r, :].rearrange("p (b m) -> p b m", m=GROUP),
+                    in0=banks[i][:].rearrange("p (b m) -> p b m", m=GROUP),
+                    in1=gates[i].unsqueeze(2).to_broadcast([P, GROUPS, GROUP]),
                     op=ALU.mult,
                 )
-                if (r + 1) % per_store == 0:
-                    first = r + 1 - per_store
-                    nc.sync.dma_start(
-                        out_rows[:, 2 * h + first : 2 * h + r + 1, c * SLOTS : (c + 1) * SLOTS], y[:, first : r + 1, :]
-                    )
+                columns = slice(c * SLOTS, (c + 1) * SLOTS)
+                if c == CHUNKS - 1 and h == 1:
+                    nc.sync.dma_start(out_rows[:, i : i + 1, columns], y[c, h][:, r : r + 1, :])
+                elif r == 1:
+                    nc.sync.dma_start(out_rows[:, i - 1 : i + 1, columns], y[c, h][:])
 
         early(0, [0, 1], "scalar")
         early(0, [2, 3], "vector")
@@ -188,17 +209,14 @@ def tile_list_group_expert_back_to_members_kernel(
         last2 = late_gather(3, 2, "p32")
         gate0 = expert(0)
         late_max(1, 2, picked1, "h0")
-        late_max(2, 1, picked2, "h0")
+        late_max(2, 1, picked2 + [last2], "h0")
         z0 = member_products(0)
-        members(0, 0, gate0, z0)
-        gate1 = expert(1, "gate0_0")
-        late_max(2, 3, [last2], "u1")
-        gate2 = expert(2)
-        members(0, 1, gate0, z0)
-        picked3 = [late_gather(1, 3, "p30"), late_gather(2, 3, "p12"), late_gather(3, 3, "h0")]
-        late_max(3, 1, picked3, "gate0_1")
+        gate1 = expert(1, "xm_w0")
+        members(0, range(N_TILES), gate0, z0)
+        gate2 = expert(2, "gate0_1")
+        picked3 = [late_gather(1, 3, "p30"), late_gather(2, 3, "p12"), late_gather(3, 3, "p32")]
+        late_max(3, 1, picked3, "gate0_0")
         gate3 = expert(3)
-        for c, gates in ((1, gate1), (2, gate2), (3, gate3)):
-            z = member_products(c)
-            members(c, 0, gates, z)
-            members(c, 1, gates, z, 1 if c == CHUNKS - 1 else 2)
+        members(1, range(N_TILES), gate1, member_products(1))
+        members(2, range(N_TILES), gate2, member_products(2))
+        members(3, range(N_TILES), gate3, member_products(3))

from contextlib import ExitStack

import concourse.mybir as mybir

K, T, J, B, N = 512, 2048, 2048, 512, 512
FLOPS = 2 * K * N * (B + J)

F32 = mybir.dt.float32
BF16 = mybir.dt.bfloat16
I32 = mybir.dt.int32
U32 = mybir.dt.uint32
U16 = mybir.dt.uint16
U8 = mybir.dt.uint8
FP8X4 = mybir.dt.float8_e4m3fn_x4
FP4X4 = mybir.dt.float4_e2m1fn_x4
ALU = mybir.AluOpType
ACT = mybir.ActivationFunctionType

P = 128
PACK = 4
GROUP = J // B
SLOTS = 512
CHUNKS = J // SLOTS
GROUPS = SLOTS // GROUP
N_TILES = N // P
LIST_COLS = SLOTS // 16


def tile_list_group_expert_back_to_members_kernel(
    tc, xf, fk, wa_words, wa_scales, xm_words, xm_scales, wm_words, wm_scales, offs, out
):
    nc = tc.nc
    with ExitStack() as ctx:
        held = ctx.enter_context(tc.tile_pool(name="held", bufs=1))
        psum_g = ctx.enter_context(tc.psum_pool(name="psum_g", bufs=2))
        psum_z = ctx.enter_context(tc.psum_pool(name="psum_z", bufs=6))

        offsets = held.tile([P, J // 16], U16, name="offsets")
        nc.sync.dma_start(offsets[:], offs)

        warm_in = held.tile([P, 1], F32, name="warm_in")
        warm_out = held.tile([P, 1], F32, name="warm_out")
        nc.vector.memset(warm_in[:], 0.0)
        nc.scalar.activation(out=warm_out[:], in_=warm_in[:], func=ACT.Sigmoid)

        wa_s = held.tile([P, N], U8, name="wa_s", align_bytes=64)
        wm_s = held.tile([P, N], U8, name="wm_s", align_bytes=64)
        xm_s = held.tile([P, J], U8, name="xm_s", align_bytes=64)
        for plane in (wa_s, wm_s, xm_s):
            nc.vector.memset(plane[:].bitcast(I32), 0)

        def load_scale_rows(queue, plane, rows):
            for q in range(4):
                queue.dma_start(plane[32 * q : 32 * q + 4, :].bitcast(I32), rows[0, 4 * q : 4 * q + 4, :].bitcast(I32))

        xf_rows = xf.rearrange("(p t) c -> p t c", t=PACK)
        x = [held.tile([P, T], F32, name=f"x{t}") for t in range(PACK)]
        for t in range(PACK):
            nc.sync.dma_start(x[t][:], xf_rows[:, t, :])
        fk_sb = held.tile([P, PACK], F32, name="fk_sb")
        wa_w = held.tile([P, 2 * N], U8, name="wa_w", align_bytes=64)
        wm_w = held.tile([P, 2 * N], U8, name="wm_w", align_bytes=64)
        load_scale_rows(nc.gpsimd, wa_s, wa_scales)
        nc.gpsimd.dma_start(fk_sb[:], fk.rearrange("(p t) o -> p (t o)", t=PACK))
        nc.sync.dma_start(wa_w[:].bitcast(I32), wa_words[0].bitcast(I32))
        nc.sync.dma_start(wm_w[:].bitcast(I32), wm_words[0].bitcast(I32))
        load_scale_rows(nc.sync, xm_s, xm_scales)
        xm_rows = xm_words[0].rearrange("p c r -> p (c r)").bitcast(I32)
        xm_w = [held.tile([P, SLOTS], I32, name=f"xm_w{c}", tag=f"xm_w{c}", align_bytes=64) for c in range(CHUNKS)]
        nc.sync.dma_start(xm_w[0][:], xm_rows[:, :SLOTS])
        load_scale_rows(nc.sync, wm_s, wm_scales)
        for c in range(1, CHUNKS):
            nc.sync.dma_start(xm_w[c][:], xm_rows[:, c * SLOTS : (c + 1) * SLOTS])

        largest = held.tile([P, CHUNKS, PACK, GROUPS], F32, name="largest")

        def gather(engine, dst, t, c, first=0, last=LIST_COLS):
            picked = x[t][:].indirect(offsets[:, c * LIST_COLS + first : c * LIST_COLS + last])
            if engine == "scalar":
                nc.scalar.activation(out=dst, in_=picked, func=ACT.Copy)
            else:
                nc.vector.tensor_copy(out=dst, in_=picked)

        def max_of_halves(dst, src):
            quads = src.rearrange("p (b m) -> p b m", m=GROUP)
            nc.vector.tensor_tensor(
                out=dst.rearrange("p (b m) -> p b m", m=2), in0=quads[:, :, 0:2], in1=quads[:, :, 2:4], op=ALU.max
            )

        def max_of_pairs(dst, src):
            pairs = src.rearrange("p (r b m) -> p r b m", r=dst.shape[1], m=2)
            nc.vector.tensor_tensor(out=dst, in0=pairs[:, :, :, 0], in1=pairs[:, :, :, 1], op=ALU.max)

        def early(t, chunks, engine):
            picked = held.tile([P, len(chunks) * SLOTS], F32, name=f"picked_{t}_{chunks[0]}")
            halves = held.tile([P, len(chunks) * SLOTS // 2], F32, name=f"halves_{t}_{chunks[0]}")
            for s, c in enumerate(chunks):
                gather(engine, picked[:, s * SLOTS : (s + 1) * SLOTS], t, c)
            max_of_halves(halves[:], picked[:])
            max_of_pairs(largest[:, chunks[0] : chunks[-1] + 1, t, :], halves[:])

        def late_gather(t, c, tag, engine="scalar"):
            picked = held.tile([P, SLOTS], F32, name=f"picked_{t}_{c}", tag=tag, align_bytes=64)
            gather(engine, picked[:], t, c)
            return picked

        def late_max(c, first, picked, tag):
            halves = held.tile([P, len(picked) * SLOTS // 2], F32, name=f"halves_late{c}_{first}", tag=tag, align_bytes=64)
            for s in range(len(picked)):
                max_of_halves(halves[:, s * SLOTS // 2 : (s + 1) * SLOTS // 2], picked[s][:])
            max_of_pairs(largest[:, c, first : first + len(picked), :], halves[:])

        def expert(c, u_tag=None):
            u = held.tile([P, GROUPS * PACK], BF16, name=f"u{c}", tag=f"u{c}", align_bytes=64)
            if c < 2:
                nc.vector.tensor_tensor(
                    out=u[:].rearrange("p (d i t) -> p d t i", i=2, t=PACK),
                    in0=largest[:, c, :, :].rearrange("p t (d i) -> p d t i", i=2),
                    in1=fk_sb[:].unsqueeze(1).unsqueeze(3).to_broadcast([P, GROUPS // 2, PACK, 2]),
                    op=ALU.mult,
                )
            elif c == 3:
                planes = held.tile([P, PACK, GROUPS], BF16, name="planes", tag="p32", align_bytes=64)
                for t in range(PACK):
                    nc.scalar.activation(
                        out=planes[:, t, :], in_=largest[:, c, t, :], func=ACT.Copy, scale=fk_sb[:, t : t + 1]
                    )
                nc.scalar.copy(out=u[:].rearrange("p (b t) -> p b t", t=PACK), in_=planes[:].rearrange("p t b -> p b t"))
            else:
                nc.gpsimd.tensor_tensor(
                    out=u[:].rearrange("p (b t) -> p b t", t=PACK),
                    in0=largest[:, c, :, :].rearrange("p t b -> p b t"),
                    in1=fk_sb[:].unsqueeze(1).to_broadcast([P, GROUPS, PACK]),
                    op=ALU.mult,
                )
            u_w = held.tile([P, GROUPS], U32, name=f"u_w{c}", tag=u_tag or f"u_w{c}", align_bytes=64)
            u_s = held.tile([P, GROUPS], U8, name=f"u_s{c}", tag=f"u_s{c}", align_bytes=64)
            nc.vector.quantize_mx(out=u_w[:].bitcast(FP8X4), scales=u_s[:], in_=u[:])
            g = psum_g.tile([P, N_TILES, GROUPS], F32, name="g")
            for i in range(N_TILES):
                nc.tensor.matmul_mx(
                    out=g[:, i, :],
                    lhsT=wa_w[:, 2 * P * i : 2 * P * (i + 1)].bitcast(FP4X4),
                    lhsT_scale=wa_s[:, P * i : P * (i + 1)],
                    rhs=u_w[:].bitcast(FP8X4),
                    rhs_scale=u_s[:],
                    start=True,
                    stop=True,
                )
            gates = []
            for h, (first, last) in enumerate(((0, 2), (2, N_TILES))):
                gate = held.tile([P, last - first, GROUPS], F32, name=f"gate{c}_{h}", tag=f"gate{c}_{h}", align_bytes=64)
                nc.scalar.activation(out=gate[:], in_=g[:, first:last, :], func=ACT.Sigmoid)
                gates.extend(gate[:, r, :] for r in range(last - first))
            return gates

        out_rows = out.rearrange("(i p) j -> p i j", p=P)

        def member_products(c):
            words = xm_w[c][:]
            banks = []
            for i in range(N_TILES):
                z = psum_z.tile([P, SLOTS], F32, name="z")
                banks.append(z)
                nc.tensor.matmul_mx(
                    out=z[:],
                    lhsT=wm_w[:, 2 * P * i : 2 * P * (i + 1)].bitcast(FP4X4),
                    lhsT_scale=wm_s[:, P * i : P * (i + 1)],
                    rhs=words.bitcast(FP8X4),
                    rhs_scale=xm_s[:, c * SLOTS : (c + 1) * SLOTS],
                    start=True,
                    stop=True,
                )
            return banks

        y = {}
        y_tags = {(1, 0): "gate0_0"}

        def members(c, tiles, gates, banks):
            for i in tiles:
                h, r = divmod(i, 2)
                if (c, h) not in y:
                    tag = y_tags.get((c, h), f"y{c}_{h}")
                    y.setdefault((c, h), held.tile([P, 2, SLOTS], F32, name=f"y{c}_{h}", tag=tag, align_bytes=64))
                nc.vector.tensor_tensor(
                    out=y[c, h][:, r, :].rearrange("p (b m) -> p b m", m=GROUP),
                    in0=banks[i][:].rearrange("p (b m) -> p b m", m=GROUP),
                    in1=gates[i].unsqueeze(2).to_broadcast([P, GROUPS, GROUP]),
                    op=ALU.mult,
                )
                columns = slice(c * SLOTS, (c + 1) * SLOTS)
                if c == CHUNKS - 1 and h == 1:
                    nc.sync.dma_start(out_rows[:, i : i + 1, columns], y[c, h][:, r : r + 1, :])
                elif r == 1:
                    nc.sync.dma_start(out_rows[:, i - 1 : i + 1, columns], y[c, h][:])

        early(0, [0, 1], "scalar")
        early(0, [2, 3], "vector")
        early(1, [0, 1], "scalar")
        picked2 = [late_gather(1, 2, "p12", "vector")]
        picked0 = [late_gather(2, 0, "p20")]
        picked1 = [late_gather(2, 1, "p21")]
        shared = held.tile([P, SLOTS], F32, name="picked_3_0", tag="p30", align_bytes=64)
        gather("scalar", shared[:, : SLOTS // 2], 3, 0, 0, LIST_COLS // 2)
        gather("vector", shared[:, SLOTS // 2 :], 3, 0, LIST_COLS // 2, LIST_COLS)
        late_max(0, 2, picked0 + [shared], "h0")
        picked1.append(late_gather(3, 1, "p31"))
        picked2.append(late_gather(2, 2, "p30"))
        last2 = late_gather(3, 2, "p32")
        gate0 = expert(0)
        late_max(1, 2, picked1, "h0")
        late_max(2, 1, picked2 + [last2], "h0")
        z0 = member_products(0)
        gate1 = expert(1, "xm_w0")
        members(0, range(N_TILES), gate0, z0)
        gate2 = expert(2, "gate0_1")
        picked3 = [late_gather(1, 3, "p30"), late_gather(2, 3, "p12"), late_gather(3, 3, "p32")]
        late_max(3, 1, picked3, "gate0_0")
        gate3 = expert(3)
        members(1, range(N_TILES), gate1, member_products(1))
        members(2, range(N_TILES), gate2, member_products(2))
        members(3, range(N_TILES), gate3, member_products(3))
